import numpy as np
import ml_dtypes


def mxq(x, axis, fmt="e4m3"):
    dtype, down = {"e4m3": (ml_dtypes.float8_e4m3fn, 7), "e5m2": (ml_dtypes.float8_e5m2, 14)}[fmt]
    v = np.moveaxis(np.asarray(x, np.float32).astype(ml_dtypes.bfloat16).astype(np.float64), axis, -1)
    blocks = v.reshape(v.shape[:-1] + (-1, 32))
    amax = np.abs(blocks).max(-1, keepdims=True)
    byte = np.maximum(np.where(amax > 0, np.frexp(amax)[1] - 1 + 127, 0) - down, 1)
    scale = np.exp2(byte - 127.0)
    codes = (blocks / scale).astype(np.float32).astype(dtype).astype(np.float64)
    return np.moveaxis((codes * scale).reshape(v.shape), -1, axis)


WIDE = False


def mx_kscale(k):
    if not WIDE:
        return np.ones(k)
    levels = np.array([10, -10, 5, -5, 0])
    if k % 512:
        return np.exp2(np.random.permutation(np.resize(levels, k // 32))).repeat(32)
    a = np.empty((k // 512, 16))
    for p in range(k // 512):
        a[p, :8] = np.random.permutation(np.resize(levels, 8))
        for g in range(8):
            far = levels[np.abs(levels - a[p, g]) >= 10]
            a[p, g + 8] = far[np.random.randint(len(far))]
    return np.exp2(a.ravel()).repeat(32)


BF16 = ml_dtypes.bfloat16


def bf(x):
    return np.asarray(x, np.float32).astype(BF16)


def f64(x):
    return np.asarray(x).astype(np.float64)


E2M1 = np.array([0.0, 0.5, 1.0, 1.5, 2.0, 3.0, 4.0, 6.0, -0.0, -0.5, -1.0, -1.5, -2.0, -3.0, -4.0, -6.0])


def pack_weight(w, fmt):
    k, n = w.shape
    w = f64(bf(w)).reshape(k // 32, 32, n)
    amax = np.abs(w).max(1)
    if fmt == "e4m3":
        byte = np.frexp(amax)[1] - 1 + 127 - 7
    else:
        mant, ex = np.frexp(amax / 6.0)
        byte = np.where(mant > 0.5, ex, ex - 1) + 127
    byte = np.clip(np.where(amax > 0, byte, 1), 1, 254)
    scaled = (w * np.exp2(127.0 - byte)[:, None, :]).reshape(k, n).astype(np.float32)
    by_word = np.ascontiguousarray(scaled.reshape(k // 512, 128, 4, n).transpose(0, 1, 3, 2))
    if fmt == "e4m3":
        words = by_word.astype(ml_dtypes.float8_e4m3fn).view(np.uint8)
    else:
        c = by_word.astype(ml_dtypes.float4_e2m1fn).view(np.uint8) & 0xF
        words = c[..., 0::2] | (c[..., 1::2] << 4)
    return np.ascontiguousarray(words), np.ascontiguousarray(byte.astype(np.uint8).reshape(k // 512, 16, n))


def unpack_weight(words, scales, fmt):
    g, p, n, _ = words.shape
    if fmt == "e4m3":
        vals = np.ascontiguousarray(words).view(ml_dtypes.float8_e4m3fn).astype(np.float64)
    else:
        nib = np.empty((g, p, n, 4), np.uint8)
        nib[..., 0::2] = words & 0xF
        nib[..., 1::2] = words >> 4
        vals = E2M1[nib]
    vals = vals * np.repeat(np.exp2(scales.astype(np.float64) - 127.0), 8, axis=1)[..., None]
    return vals.transpose(0, 1, 3, 2).reshape(g * 512, n)
def pack4(w):
    words, scales = pack_weight(w, "e2m1")
    return words.reshape(words.shape[0], 128, -1), scales


def unpack4(words, scales):
    return unpack_weight(words.reshape(words.shape[0], 128, -1, 2), scales, "e2m1")


B, S, L, W, D, F, R = 16, 64, 72, 9, 1024, 1024, 256


def silu(v):
    return v / (1.0 + np.exp(-v))


def draw0():
    s, t = mx_kscale(D), mx_kscale(F)
    ws_words, ws_scales = pack4(np.random.standard_normal((D, F)) / np.sqrt(D) / s[:, None])
    we_words, we_scales = pack4(np.random.standard_normal((D, F)) / np.sqrt(D) / s[:, None])
    wv_words, wv_scales = pack4(np.random.standard_normal((F, R)) / np.sqrt(F) / t[:, None])
    return {"x": bf(np.random.standard_normal((B, L, D)) * s),
            "ws_words": ws_words, "ws_scales": ws_scales,
            "we_words": we_words, "we_scales": we_scales,
            "width": bf(0.5 * np.random.standard_normal((W, F))),
            "gain": bf((1.0 + 0.1 * np.random.standard_normal(F)) * t),
            "wv_words": wv_words, "wv_scales": wv_scales,
            "prior": bf(0.3 * np.random.standard_normal((W, R)))}


def core(x, ws_words, ws_scales, we_words, we_scales, width, gain, wv_words, wv_scales, prior):
    xq = mxq(f64(x), 2, "e4m3")
    a = (xq[:, :S].reshape(B * S, D) @ unpack4(ws_words, ws_scales)).reshape(B, S, F)
    e = (xq.reshape(B * L, D) @ unpack4(we_words, we_scales)).reshape(B, L, F)
    wd = f64(width)
    v = np.stack([a + e[:, w:w + S] + wd[w] for w in range(W)], axis=2)
    z = silu(v)
    h = z / np.sqrt(np.mean(z * z, axis=3, keepdims=True)) * f64(gain)
    y = mxq(h.reshape(B * S * W, F), 1, "e4m3") @ unpack4(wv_words, wv_scales)
    return y.reshape(B, S, W, R) + f64(prior)


def e4m3fn_bytes(y):
    return np.clip(np.asarray(y, np.float64), -448.0, 448.0).astype(np.float32).astype(ml_dtypes.float8_e4m3fn).view(np.uint8)


def e4m3fn_values(b):
    return np.asarray(b, np.uint8).view(ml_dtypes.float8_e4m3fn).astype(np.float64)


def setup_inputs():
    d = draw0()
    x0 = np.asarray(d['x']).astype(np.float64)
    s = (np.max(np.abs(x0), axis=(0, 1), keepdims=True) / 448.0).astype(np.float32)
    out = {}
    for k, v in d.items():
        if k == 'x':
            out['x_bytes'] = e4m3fn_bytes(x0 / s.astype(np.float64))
            out['x_scale'] = s
        else:
            out[k] = v
    return out


def reference(x_bytes, x_scale, ws_words, ws_scales, we_words, we_scales, width, gain, wv_words, wv_scales, prior):
    return core(e4m3fn_values(x_bytes) * x_scale.astype(np.float64), ws_words, ws_scales, we_words, we_scales, width, gain, wv_words, wv_scales, prior)

@@ -1,0 +1,389 @@
+from contextlib import ExitStack
+
+import concourse.mybir as mybir
+from concourse.masks import make_identity
+
+F32 = mybir.dt.float32
+BF16 = mybir.dt.bfloat16
+I32 = mybir.dt.int32
+U32 = mybir.dt.uint32
+U8 = mybir.dt.uint8
+FP8 = mybir.dt.float8_e4m3fn
+FP8X4 = mybir.dt.float8_e4m3fn_x4
+FP4X4 = mybir.dt.float4_e2m1fn_x4
+ACT = mybir.ActivationFunctionType
+ALU = mybir.AluOpType
+
+B, S, L, W, D, F, R = 16, 64, 72, 9, 1024, 1024, 256
+FLOPS = 2 * (B * S * D * F + B * L * D * F + B * S * W * F * R)
+
+P = 128
+KG = 2
+CH = 8
+TOK = L * B
+HALF = 512
+GROUPS = [(h, w) for h in range(2) for w in range(W)]
+NG = len(GROUPS)
+PE_CHUNKS = (1, 5, 7)
+GP_CHUNKS = (0, 2, 3, 4, 6)
+HEAD = [("ae",0,"sss"),("v",1),("ae",2,"sss"),("ae",3,"ssv"),("s",1),("s",0),("ae",4,"vvv"),("s",2),("s",3),("ae",6,"vvv"),("v",5),("s",4),("s",5),("v",7),("s",6),("s",7)]
+GAIN_G = (0, 1, 2, 3)
+GAIN_V = (4, 5, 6, 7)
+
+
+def tile_endpoint_span_scorer_f1_kernel(
+    tc, x_bytes, x_scale, ws_words, ws_scales, we_words, we_scales, width, gain, wv_words, wv_scales, prior, out
+):
+    nc = tc.nc
+    with ExitStack() as ctx:
+        keep = ctx.enter_context(tc.tile_pool(name="keep", bufs=1))
+        work = ctx.enter_context(tc.tile_pool(name="work", bufs=2))
+        psum = ctx.enter_context(tc.psum_pool(name="psum", bufs=1))
+        ctx.enter_context(tc.manual_schedule())
+
+        ident = keep.tile([P, P], F32, name="ident")
+        warm = keep.tile([P, 1], F32, name="warm")
+        mhalf = keep.tile([P, 4], F32, name="mhalf")
+        xsc = keep.tile([P, D], F32, name="xsc")
+        ws_raw = keep.tile([P, KG, 2048], U8, name="ws_raw")
+        we_raw = keep.tile([P, KG, 2048], U8, name="we_raw")
+        wss_raw = keep.tile([P, KG, F], U8, name="wss_raw")
+        wes_raw = keep.tile([P, KG, F], U8, name="wes_raw")
+        wsp = keep.tile([P, KG, 2048], U8, name="wsp", align_bytes=64)
+        wep = keep.tile([P, KG, 2048], U8, name="wep", align_bytes=64)
+        wssp = keep.tile([P, KG, F], U8, name="wssp", align_bytes=64)
+        wesp = keep.tile([P, KG, F], U8, name="wesp", align_bytes=64)
+        wv = keep.tile([P, KG, 512], U8, name="wv", align_bytes=64)
+        wvs = keep.tile([P, KG, R], U8, name="wvs", align_bytes=64)
+        xt = keep.tile([P, KG, TOK * 4], BF16, name="xt", align_bytes=64)
+        xc = keep.tile([P, KG, TOK], U32, name="xc", align_bytes=64)
+        xp = [keep.tile([P, KG, TOK], U8, name="xp%d" % s, align_bytes=64) for s in range(4)]
+        wg = keep.tile([P, F], BF16, name="wg")
+        wgt = keep.tile([P, KG, 16, 2], F32, name="wgt")
+        wid = keep.tile([P, CH, W], F32, name="wid")
+        g32 = keep.tile([P, CH], F32, name="g32")
+        pr = keep.tile([P, W, R], BF16, name="pr")
+        a_sb = keep.tile([P, len(GP_CHUNKS), S * B], F32, name="a_sb")
+        e_sb = keep.tile([P, len(GP_CHUNKS), TOK], F32, name="e_sb")
+
+        nc.scalar.dma_start(out=xsc[:], in_=x_scale.rearrange("a o k -> (a o k)").partition_broadcast(P))
+        xb = []
+
+        def load_x(m):
+            t = keep.tile([P, D], U8, name="xb%d" % m)
+            nc.sync.dma_start(out=t[:], in_=x_bytes[:, 8 * m : 8 * m + 8, :].rearrange("b j d -> j b d"))
+            xb.append(t)
+
+        def load_words(tile, src):
+            nc.sync.dma_start(out=tile[:].bitcast(I32), in_=src.rearrange("g p n -> p g n").bitcast(I32))
+
+        def load_scales(tile, src):
+            for q in range(4):
+                nc.sync.dma_start(
+                    out=tile[32 * q : 32 * q + 4, :, :].bitcast(I32),
+                    in_=src[:, 4 * q : 4 * q + 4, :].rearrange("g q n -> q g n").bitcast(I32),
+                )
+
+        for t in (wss_raw, wes_raw, wvs, xp[0]):
+            nc.vector.memset(t[:].bitcast(I32), 0)
+        nc.gpsimd.memset(warm[:], 0.0)
+        nc.gpsimd.memset(mhalf[:], -0.5)
+        nc.gpsimd.memset(wg[:], 0.0)
+        make_identity(nc, ident[:])
+        nc.scalar.activation(out=warm[:], in_=warm[:], func=ACT.Silu)
+
+        for m in range(5):
+            load_x(m)
+        nc.sync.dma_start(out=wg[0:W, :], in_=width)
+        nc.sync.dma_start(out=wg[W : W + 1, :], in_=gain.unsqueeze(0))
+        load_words(we_raw, we_words)
+        load_words(ws_raw, ws_words)
+        load_scales(wes_raw, we_scales)
+        load_scales(wss_raw, ws_scales)
+        for m in range(5, 9):
+            load_x(m)
+        load_words(wv, wv_words)
+        load_scales(wvs, wv_scales)
+        nc.sync.dma_start(out=pr[:].rearrange("p w r -> p (w r)"), in_=prior.rearrange("w r -> (w r)").partition_broadcast(P))
+
+        def x_tile(m):
+            xs = work.tile([P, D], BF16, name="xs", tag="xs", bufs=3)
+            nc.vector.tensor_tensor(out=xs[:], in0=xb[m][:].bitcast(FP8), in1=xsc[:], op=ALU.mult)
+            words = xs[:].bitcast(F32)
+            bank = psum.tile([P, 4, P], F32, name="zt", tag="zt", bufs=3)
+            for g in range(KG):
+                for u in range(2):
+                    nc.tensor.transpose(bank[:, 2 * g + u, :], words[:, 256 * g + u : 256 * (g + 1) : 2], ident[:])
+            nc.scalar.copy(
+                out=xt[:].bitcast(F32)[:, :, 256 * m : 256 * (m + 1)].rearrange("p g (n u) -> p g n u", u=2),
+                in_=bank[:].rearrange("p (g u) n -> p g n u", u=2),
+            )
+
+        def x_quant(n0, n1):
+            for g in range(KG):
+                nc.vector.quantize_mx(
+                    out=xc[:, g, n0:n1].bitcast(FP8X4),
+                    scales=xp[0][:, g, n0:n1],
+                    in_=xt[:, g, 4 * n0 : 4 * n1],
+                )
+
+        def shift_planes(n0, n1):
+            for s in range(1, 4):
+                lo = max(n0, 16 * s)
+                nc.vector.tensor_copy(
+                    out=xp[s][:, :, lo - 16 * s : n1 - 16 * s].bitcast(I32),
+                    in_=xp[0][:, :, lo:n1].bitcast(I32),
+                )
+
+        def perm_words(dst, src, fg):
+            for g in range(KG):
+                nc.vector.tensor_copy(
+                    out=dst[:, g, 1024 * fg : 1024 * (fg + 1)].rearrange("p (t m b) -> p t m b", t=4, b=2),
+                    in_=src[:, g, 1024 * fg : 1024 * (fg + 1)].rearrange("p (m t b) -> p t m b", t=4, b=2),
+                )
+
+        def perm_scales(dst, src, fg):
+            nc.vector.tensor_copy(
+                out=dst[:, :, 512 * fg : 512 * (fg + 1)].rearrange("p g (t m) -> p g t m", t=4),
+                in_=src[:, :, 512 * fg : 512 * (fg + 1)].rearrange("p g (m t) -> p g t m", t=4),
+            )
+
+        def proj(bank, words, scales, c, n0, n, plane, first, last):
+            for g in range(KG):
+                nc.tensor.matmul_mx(
+                    out=bank,
+                    lhsT=words[:, g, 256 * c : 256 * (c + 1)].bitcast(FP4X4),
+                    lhsT_scale=scales[:, g, P * c : P * (c + 1)],
+                    rhs=xc[:, g, n0 : n0 + n].bitcast(FP8X4),
+                    rhs_scale=xp[plane][:, g, n0 - 16 * plane : n0 - 16 * plane + n],
+                    start=(first and g == 0),
+                    stop=(last and g == KG - 1),
+                )
+
+        def evac(eng, dst, src):
+            if eng == "s":
+                nc.scalar.copy(out=dst, in_=src)
+            else:
+                nc.vector.tensor_copy(out=dst, in_=src)
+
+        def proj_ae(c, half, engines):
+            gi = GP_CHUNKS.index(c)
+            spans = [(0, 512), (512, 128)] if half == 0 else [(640, 512)]
+            bank = psum.tile([P, HALF], F32, name="vp", tag="vp", bufs=2)
+            proj(bank[:], wsp, wssp, c, HALF * half, HALF, 0, True, True)
+            evac(engines[0], a_sb[:, gi, HALF * half : HALF * (half + 1)], bank[:])
+            for i, (n0, n) in enumerate(spans):
+                bank = psum.tile([P, HALF], F32, name="vp", tag="vp", bufs=2)
+                proj(bank[:, :n], wep, wesp, c, n0, n, 0, True, True)
+                evac(engines[1 + i], e_sb[:, gi, n0 : n0 + n], bank[:, :n])
+
+        v = {}
+        vbank = {}
+        z = {}
+        ss = {}
+        rb = {}
+        rs = {}
+        hb = {}
+        hc = {}
+        hs = {}
+
+        def ok(k):
+            return 0 <= k < NG
+
+        def vadd(k, c):
+            half, w = GROUPS[k]
+            gi = GP_CHUNKS.index(c)
+            if gi == 0:
+                v[k] = work.tile([P, len(GP_CHUNKS), HALF], F32, name="v", tag="v", bufs=2)
+            n0 = HALF * half
+            nc.gpsimd.tensor_tensor(
+                out=v[k][:, gi, :],
+                in0=a_sb[:, gi, n0 : n0 + HALF],
+                in1=e_sb[:, gi, n0 + B * w : n0 + B * w + HALF],
+                op=ALU.add,
+            )
+
+        def vpe(k, c):
+            half, w = GROUPS[k]
+            bank = psum.tile([P, HALF], F32, name="vp", tag="vp", bufs=2)
+            proj(bank[:], wsp, wssp, c, HALF * half, HALF, 0, True, False)
+            proj(bank[:], wep, wesp, c, HALF * half + B * w, HALF, w % 4, False, True)
+            vbank[k, c] = bank
+
+        def silu(k, c):
+            half, w = GROUPS[k]
+            if k not in z:
+                z[k] = work.tile([P, CH, HALF], F32, name="z", tag="z", bufs=3)
+            src = vbank.pop((k, c))[:] if c in PE_CHUNKS else v[k][:, GP_CHUNKS.index(c), :]
+            nc.scalar.activation(out=z[k][:, c, :], in_=src, func=ACT.Silu, bias=wid[:, c, w : w + 1])
+
+        zbank = {}
+
+        def ztr(k, i):
+            q, j = divmod(i, 4)
+            bank = psum.tile([P, 4, P], F32, name="zt", tag="zt", bufs=3)
+            for t in range(4):
+                nc.tensor.transpose(bank[:, t, :], z[k][:, 4 * q + t, P * j : P * (j + 1)], ident[:])
+            zbank[k, i] = bank
+
+        def square(k, i):
+            q, j = divmod(i, 4)
+            if i == 0:
+                ss[k] = work.tile([P, 2, 4], F32, name="ss", tag="ss", bufs=3)
+            junk = work.tile([P, HALF], BF16, name="junk", tag="junk", bufs=2)
+            nc.scalar.activation(
+                out=junk[:],
+                in_=zbank.pop((k, i))[:].rearrange("p t n -> p (t n)"),
+                func=ACT.Square,
+                accum_out=ss[k][:, q, j : j + 1],
+            )
+
+        def rstd(k):
+            tot = work.tile([P, 4], F32, name="tot", tag="tot", bufs=2)
+            nc.gpsimd.tensor_tensor(out=tot[:], in0=ss[k][:, 0, :], in1=ss[k][:, 1, :], op=ALU.add)
+            rs[k] = work.tile([P, 4], F32, name="rs", tag="rs", bufs=2)
+            nc.gpsimd.tensor_tensor(out=rs[k][:], in0=tot[:], in1=mhalf[:], op=ALU.pow)
+
+        def spread(k):
+            bank = psum.tile([P, HALF], F32, name="rb", tag="rb", bufs=1)
+            for j in range(4):
+                nc.tensor.transpose(bank[:, P * j : P * (j + 1)], rs[k][:, j : j + 1].to_broadcast([P, P]), ident[:])
+            rb[k] = bank
+
+        def gain_g(k, c):
+            nc.gpsimd.tensor_scalar(
+                out=z[k][:, c, :], in0=z[k][:, c, :], scalar1=g32[:, c : c + 1], scalar2=0.0, op0=ALU.mult, op1=ALU.add
+            )
+
+        def gain_v(k, c):
+            nc.vector.tensor_scalar(
+                out=z[k][:, c, :], in0=z[k][:, c, :], scalar1=g32[:, c : c + 1], scalar2=None, op0=ALU.mult
+            )
+
+        def norm(k, g):
+            if g == 0:
+                hb[k] = work.tile([P, KG, 4 * HALF], BF16, name="hb", tag="hb", bufs=2, align_bytes=64)
+            nc.vector.tensor_tensor(
+                out=hb[k][:, g, :].rearrange("p (c i t) -> p c t i", i=4, t=4),
+                in0=z[k][:, 4 * g : 4 * g + 4, :].rearrange("p t (c i) -> p c t i", i=4),
+                in1=rb[k][:].rearrange("p (c i) -> p c i", i=4).unsqueeze(2).to_broadcast([P, P, 4, 4]),
+                op=ALU.mult,
+            )
+
+        def quant(k, g):
+            if g == 0:
+                hc[k] = work.tile([P, KG, HALF], U32, name="hc", tag="hc", bufs=2, align_bytes=64)
+                hs[k] = work.tile([P, KG, HALF], U8, name="hs", tag="hs", bufs=2, align_bytes=64)
+            nc.vector.quantize_mx(out=hc[k][:, g, :].bitcast(FP8X4), scales=hs[k][:, g, :], in_=hb[k][:, g, :])
+
+        obank = {}
+
+        def outmm(k, jj):
+            bank = psum.tile([P, 2, R], F32, name="o", tag="o", bufs=2)
+            for j2 in range(2):
+                j = 2 * jj + j2
+                for rh in range(2):
+                    for g in range(KG):
+                        nc.tensor.matmul_mx(
+                            out=bank[:, j2, P * rh : P * (rh + 1)],
+                            lhsT=hc[k][:, g, P * j : P * (j + 1)].bitcast(FP8X4),
+                            lhsT_scale=hs[k][:, g, P * j : P * (j + 1)],
+                            rhs=wv[:, g, 2 * P * rh : 2 * P * (rh + 1)].bitcast(FP4X4),
+                            rhs_scale=wvs[:, g, P * rh : P * (rh + 1)],
+                            start=(g == 0),
+                            stop=(g == KG - 1),
+                        )
+            obank[k, jj] = bank
+
+        def finish(k, jj):
+            half, w = GROUPS[k]
+            so = work.tile([P, 2, R], F32, name="so", tag="so", bufs=4)
+            nc.vector.tensor_tensor(
+                out=so[:], in0=obank.pop((k, jj))[:], in1=pr[:, w, :].unsqueeze(1).to_broadcast([P, 2, R]), op=ALU.add
+            )
+            for j2 in range(2):
+                i0 = 32 * half + 8 * (2 * jj + j2)
+                nc.sync.dma_start(out=out[:, i0 : i0 + 8, w, :].rearrange("b i r -> i b r"), in_=so[:, j2, :])
+
+        for m in range(5):
+            x_tile(m)
+        bank = psum.tile([P, 4, P], F32, name="zt", tag="zt", bufs=3)
+        words = wg[:].bitcast(F32)
+        for g in range(KG):
+            for u in range(2):
+                nc.tensor.transpose(bank[:, 2 * g + u, :], words[:, 256 * g + u : 256 * (g + 1) : 2], ident[:])
+        nc.scalar.copy(out=wgt[:], in_=bank[:, :, 0:16].rearrange("p (g u) n -> p g n u", u=2))
+        perm_words(wsp, ws_raw, 0)
+        perm_scales(wssp, wss_raw, 0)
+        x_quant(0, 512)
+        perm_words(wep, we_raw, 0)
+        perm_scales(wesp, wes_raw, 0)
+        x_quant(512, 640)
+        wgt_bf = wgt[:].rearrange("p g n u -> p (g n u)").bitcast(BF16).rearrange("p (g n t) -> p g n t", g=2, t=4)
+        for g in range(KG):
+            nc.vector.tensor_copy(out=wid[:, 4 * g : 4 * g + 4, :], in_=wgt_bf[:, g, 0:W, :].rearrange("p n t -> p t n"))
+        perm_words(wsp, ws_raw, 1)
+        perm_scales(wssp, wss_raw, 1)
+        perm_words(wep, we_raw, 1)
+        perm_scales(wesp, wes_raw, 1)
+        for g in range(KG):
+            nc.vector.tensor_scalar(
+                out=g32[:, 4 * g : 4 * g + 4], in0=wgt_bf[:, g, W, :], scalar1=32.0, scalar2=None, op0=ALU.mult
+            )
+        shift_planes(0, 640)
+        for step in HEAD:
+            c = step[1]
+            if step[0] == "ae":
+                proj_ae(c, 0, step[2])
+                vadd(0, c)
+            if step[0] == "v":
+                vpe(0, c)
+            if step[0] == "s":
+                silu(0, c)
+        for c in GP_CHUNKS:
+            vadd(1, c)
+
+        for k in range(NG + 2):
+            for c in GP_CHUNKS[:1]:
+                if ok(k + 2):
+                    vadd(k + 2, c)
+            if ok(k - 1):
+                rstd(k - 1)
+            for c in GP_CHUNKS[1:]:
+                if ok(k + 2):
+                    vadd(k + 2, c)
+            if ok(k - 1):
+                for c in GAIN_V:
+                    gain_v(k - 1, c)
+            for i in range(8):
+                if ok(k) and i % 2 == 0:
+                    ztr(k, i)
+                    ztr(k, i + 1)
+                if i == 2 and ok(k - 1):
+                    spread(k - 1)
+                    norm(k - 1, 0)
+                    norm(k - 1, 1)
+                if i == 2 and ok(k - 2):
+                    outmm(k - 2, 0)
+                    outmm(k - 2, 1)
+                    finish(k - 2, 0)
+                    finish(k - 2, 1)
+                if ok(k + 1) and i in PE_CHUNKS:
+                    vpe(k + 1, i)
+                if k == 0 and i % 2 == 1:
+                    x_tile(5 + i // 2)
+                if ok(k):
+                    square(k, i)
+                if ok(k + 1):
+                    silu(k + 1, i)
+            if k == 0:
+                x_quant(640, 1152)
+                shift_planes(640, 1152)
+            if 1 <= k <= len(GP_CHUNKS):
+                proj_ae(GP_CHUNKS[k - 1], 1, "vv")
+            if ok(k - 1):
+                quant(k - 1, 0)
+                quant(k - 1, 1)
+            if ok(k):
+                for c in GAIN_G:
+                    gain_g(k, c)

@@ -24,11 +24,11 @@ TOK = L * B
 HALF = 512
 GROUPS = [(h, w) for h in range(2) for w in range(W)]
 NG = len(GROUPS)
-PE_CHUNKS = (1, 5, 7)
-GP_CHUNKS = (0, 2, 3, 4, 6)
-HEAD = [("ae",0,"sss"),("v",1),("ae",2,"sss"),("ae",3,"ssv"),("s",1),("s",0),("ae",4,"vvv"),("s",2),("s",3),("ae",6,"vvv"),("v",5),("s",4),("s",5),("v",7),("s",6),("s",7)]
-GAIN_G = (0, 1, 2, 3)
-GAIN_V = (4, 5, 6, 7)
+PE_CHUNKS = (1, 3, 5, 7)
+GP_CHUNKS = (0, 2, 4, 6)
+HEAD = [("ae",0,"sss"),("v",1),("ae",2,"sss"),("v",3),("s",1),("s",0),("ae",4,"ssv"),("s",2),("s",3),("ae",6,"vvv"),("v",5),("s",4),("s",5),("v",7),("s",6),("s",7)]
+GAIN_G = ()
+GAIN_V = (0, 1, 2, 3, 4, 5, 6, 7)
 
 
 def tile_endpoint_span_scorer_f1_kernel(
@@ -196,7 +196,7 @@ def tile_endpoint_span_scorer_f1_kernel(
             if gi == 0:
                 v[k] = work.tile([P, len(GP_CHUNKS), HALF], F32, name="v", tag="v", bufs=2)
             n0 = HALF * half
-            nc.gpsimd.tensor_tensor(
+            nc.vector.tensor_tensor(
                 out=v[k][:, gi, :],
                 in0=a_sb[:, gi, n0 : n0 + HALF],
                 in1=e_sb[:, gi, n0 + B * w : n0 + B * w + HALF],
@@ -344,16 +344,9 @@ def tile_endpoint_span_scorer_f1_kernel(
             vadd(1, c)
 
         for k in range(NG + 2):
-            for c in GP_CHUNKS[:1]:
-                if ok(k + 2):
-                    vadd(k + 2, c)
             if ok(k - 1):
                 rstd(k - 1)
-            for c in GP_CHUNKS[1:]:
-                if ok(k + 2):
-                    vadd(k + 2, c)
-            if ok(k - 1):
-                for c in GAIN_V:
+                for c in range(4, 8):
                     gain_v(k - 1, c)
             for i in range(8):
                 if ok(k) and i % 2 == 0:
@@ -362,12 +355,15 @@ def tile_endpoint_span_scorer_f1_kernel(
                 if i == 2 and ok(k - 1):
                     spread(k - 1)
                     norm(k - 1, 0)
-                    norm(k - 1, 1)
-                if i == 2 and ok(k - 2):
+                if i == 3 and ok(k - 2):
                     outmm(k - 2, 0)
                     outmm(k - 2, 1)
                     finish(k - 2, 0)
                     finish(k - 2, 1)
+                if i % 2 == 1 and ok(k + 2):
+                    vadd(k + 2, i - 1)
+                if i == 4 and ok(k - 1):
+                    norm(k - 1, 1)
                 if ok(k + 1) and i in PE_CHUNKS:
                     vpe(k + 1, i)
                 if k == 0 and i % 2 == 1:
@@ -376,6 +372,9 @@ def tile_endpoint_span_scorer_f1_kernel(
                     square(k, i)
                 if ok(k + 1):
                     silu(k + 1, i)
+                if i == 6 and ok(k):
+                    for c in range(4):
+                        gain_v(k, c)
             if k == 0:
                 x_quant(640, 1152)
                 shift_planes(640, 1152)
@@ -384,6 +383,3 @@ def tile_endpoint_span_scorer_f1_kernel(
             if ok(k - 1):
                 quant(k - 1, 0)
                 quant(k - 1, 1)
-            if ok(k):
-                for c in GAIN_G:
-                    gain_g(k, c)

@@ -27,8 +27,6 @@ NG = len(GROUPS)
 PE_CHUNKS = (1, 3, 5, 7)
 GP_CHUNKS = (0, 2, 4, 6)
 HEAD = [("ae",0,"sss"),("v",1),("ae",2,"sss"),("v",3),("s",1),("s",0),("ae",4,"ssv"),("s",2),("s",3),("ae",6,"vvv"),("v",5),("s",4),("s",5),("v",7),("s",6),("s",7)]
-GAIN_G = ()
-GAIN_V = (0, 1, 2, 3, 4, 5, 6, 7)
 
 
 def tile_endpoint_span_scorer_f1_kernel(
@@ -106,11 +104,15 @@ def tile_endpoint_span_scorer_f1_kernel(
         load_scales(wvs, wv_scales)
         nc.sync.dma_start(out=pr[:].rearrange("p w r -> p (w r)"), in_=prior.rearrange("w r -> (w r)").partition_broadcast(P))
 
-        def x_tile(m):
-            xs = work.tile([P, D], BF16, name="xs", tag="xs", bufs=3)
-            nc.vector.tensor_tensor(out=xs[:], in0=xb[m][:].bitcast(FP8), in1=xsc[:], op=ALU.mult)
-            words = xs[:].bitcast(F32)
-            bank = psum.tile([P, 4, P], F32, name="zt", tag="zt", bufs=3)
+        xs = {}
+
+        def x_prod(m):
+            xs[m] = work.tile([P, D], BF16, name="xs", tag="xs", bufs=4)
+            nc.vector.tensor_tensor(out=xs[m][:], in0=xb[m][:].bitcast(FP8), in1=xsc[:], op=ALU.mult)
+
+        def x_turn(m):
+            words = xs.pop(m)[:].bitcast(F32)
+            bank = psum.tile([P, 4, P], F32, name="o", tag="o", bufs=2)
             for g in range(KG):
                 for u in range(2):
                     nc.tensor.transpose(bank[:, 2 * g + u, :], words[:, 256 * g + u : 256 * (g + 1) : 2], ident[:])
@@ -184,19 +186,20 @@ def tile_endpoint_span_scorer_f1_kernel(
         rb = {}
         rs = {}
         hb = {}
+        hp = {}
         hc = {}
         hs = {}
 
         def ok(k):
             return 0 <= k < NG
 
-        def vadd(k, c):
+        def vadd(k, c, eng=nc.gpsimd):
             half, w = GROUPS[k]
             gi = GP_CHUNKS.index(c)
             if gi == 0:
                 v[k] = work.tile([P, len(GP_CHUNKS), HALF], F32, name="v", tag="v", bufs=2)
             n0 = HALF * half
-            nc.vector.tensor_tensor(
+            eng.tensor_tensor(
                 out=v[k][:, gi, :],
                 in0=a_sb[:, gi, n0 : n0 + HALF],
                 in1=e_sb[:, gi, n0 + B * w : n0 + B * w + HALF],
@@ -240,7 +243,7 @@ def tile_endpoint_span_scorer_f1_kernel(
 
         def rstd(k):
             tot = work.tile([P, 4], F32, name="tot", tag="tot", bufs=2)
-            nc.gpsimd.tensor_tensor(out=tot[:], in0=ss[k][:, 0, :], in1=ss[k][:, 1, :], op=ALU.add)
+            nc.vector.tensor_tensor(out=tot[:], in0=ss[k][:, 0, :], in1=ss[k][:, 1, :], op=ALU.add)
             rs[k] = work.tile([P, 4], F32, name="rs", tag="rs", bufs=2)
             nc.gpsimd.tensor_tensor(out=rs[k][:], in0=tot[:], in1=mhalf[:], op=ALU.pow)
 
@@ -250,25 +253,22 @@ def tile_endpoint_span_scorer_f1_kernel(
                 nc.tensor.transpose(bank[:, P * j : P * (j + 1)], rs[k][:, j : j + 1].to_broadcast([P, P]), ident[:])
             rb[k] = bank
 
-        def gain_g(k, c):
-            nc.gpsimd.tensor_scalar(
-                out=z[k][:, c, :], in0=z[k][:, c, :], scalar1=g32[:, c : c + 1], scalar2=0.0, op0=ALU.mult, op1=ALU.add
+        def norm(k, c):
+            if c == 0:
+                hp[k] = work.tile([P, CH, HALF], BF16, name="hp", tag="hp", bufs=2)
+            nc.vector.scalar_tensor_tensor(
+                out=hp[k][:, c, :], in0=z[k][:, c, :], scalar=g32[:, c : c + 1], in1=rb[k][:], op0=ALU.mult, op1=ALU.mult
             )
 
-        def gain_v(k, c):
-            nc.vector.tensor_scalar(
-                out=z[k][:, c, :], in0=z[k][:, c, :], scalar1=g32[:, c : c + 1], scalar2=None, op0=ALU.mult
-            )
-
-        def norm(k, g):
+        def weave(k, g, eng="v"):
             if g == 0:
                 hb[k] = work.tile([P, KG, 4 * HALF], BF16, name="hb", tag="hb", bufs=2, align_bytes=64)
-            nc.vector.tensor_tensor(
-                out=hb[k][:, g, :].rearrange("p (c i t) -> p c t i", i=4, t=4),
-                in0=z[k][:, 4 * g : 4 * g + 4, :].rearrange("p t (c i) -> p c t i", i=4),
-                in1=rb[k][:].rearrange("p (c i) -> p c i", i=4).unsqueeze(2).to_broadcast([P, P, 4, 4]),
-                op=ALU.mult,
-            )
+            dst = hb[k][:, g, :].rearrange("p (c i t) -> p c t i", i=4, t=4)
+            src = hp[k][:, 4 * g : 4 * g + 4, :].rearrange("p t (c i) -> p c t i", i=4)
+            if eng == "v":
+                nc.vector.tensor_copy(out=dst, in_=src)
+            else:
+                nc.scalar.copy(out=dst, in_=src)
 
         def quant(k, g):
             if g == 0:
@@ -297,7 +297,7 @@ def tile_endpoint_span_scorer_f1_kernel(
 
         def finish(k, jj):
             half, w = GROUPS[k]
-            so = work.tile([P, 2, R], F32, name="so", tag="so", bufs=4)
+            so = work.tile([P, 2, R], F32, name="so", tag="so", bufs=3)
             nc.vector.tensor_tensor(
                 out=so[:], in0=obank.pop((k, jj))[:], in1=pr[:, w, :].unsqueeze(1).to_broadcast([P, 2, R]), op=ALU.add
             )
@@ -306,7 +306,8 @@ def tile_endpoint_span_scorer_f1_kernel(
                 nc.sync.dma_start(out=out[:, i0 : i0 + 8, w, :].rearrange("b i r -> i b r"), in_=so[:, j2, :])
 
         for m in range(5):
-            x_tile(m)
+            x_prod(m)
+            x_turn(m)
         bank = psum.tile([P, 4, P], F32, name="zt", tag="zt", bufs=3)
         words = wg[:].bitcast(F32)
         for g in range(KG):
@@ -335,51 +336,50 @@ def tile_endpoint_span_scorer_f1_kernel(
             c = step[1]
             if step[0] == "ae":
                 proj_ae(c, 0, step[2])
-                vadd(0, c)
+                vadd(0, c, nc.vector)
             if step[0] == "v":
                 vpe(0, c)
             if step[0] == "s":
                 silu(0, c)
         for c in GP_CHUNKS:
-            vadd(1, c)
+            vadd(1, c, nc.vector)
+        for m in range(5, 9):
+            x_prod(m)
 
-        for k in range(NG + 2):
+        for k in range(NG + 3):
             if ok(k - 1):
                 rstd(k - 1)
-                for c in range(4, 8):
-                    gain_v(k - 1, c)
+            if ok(k + 2):
+                for c in GP_CHUNKS:
+                    vadd(k + 2, c)
+            if ok(k - 3):
+                finish(k - 3, 0)
+                finish(k - 3, 1)
             for i in range(8):
                 if ok(k) and i % 2 == 0:
                     ztr(k, i)
                     ztr(k, i + 1)
                 if i == 2 and ok(k - 1):
                     spread(k - 1)
-                    norm(k - 1, 0)
-                if i == 3 and ok(k - 2):
+                    for c in range(CH):
+                        norm(k - 1, c)
+                    for g in range(KG):
+                        weave(k - 1, g, "s" if k == NG and g == 0 else "v")
+                    for g in range(KG):
+                        quant(k - 1, g)
+                if i == 5 and ok(k - 2):
                     outmm(k - 2, 0)
                     outmm(k - 2, 1)
-                    finish(k - 2, 0)
-                    finish(k - 2, 1)
-                if i % 2 == 1 and ok(k + 2):
-                    vadd(k + 2, i - 1)
-                if i == 4 and ok(k - 1):
-                    norm(k - 1, 1)
                 if ok(k + 1) and i in PE_CHUNKS:
                     vpe(k + 1, i)
                 if k == 0 and i % 2 == 1:
-                    x_tile(5 + i // 2)
+                    x_turn(5 + i // 2)
                 if ok(k):
                     square(k, i)
                 if ok(k + 1):
                     silu(k + 1, i)
-                if i == 6 and ok(k):
-                    for c in range(4):
-                        gain_v(k, c)
-            if k == 0:
+            if k == 1:
                 x_quant(640, 1152)
                 shift_planes(640, 1152)
-            if 1 <= k <= len(GP_CHUNKS):
-                proj_ae(GP_CHUNKS[k - 1], 1, "vv")
-            if ok(k - 1):
-                quant(k - 1, 0)
-                quant(k - 1, 1)
+            if 2 <= k <= 1 + len(GP_CHUNKS):
+                proj_ae(GP_CHUNKS[k - 2], 1, "vs")

@@ -24,9 +24,13 @@ TOK = L * B
 HALF = 512
 GROUPS = [(h, w) for h in range(2) for w in range(W)]
 NG = len(GROUPS)
-PE_CHUNKS = (1, 3, 5, 7)
-GP_CHUNKS = (0, 2, 4, 6)
-HEAD = [("ae",0,"sss"),("v",1),("ae",2,"sss"),("v",3),("s",1),("s",0),("ae",4,"ssv"),("s",2),("s",3),("ae",6,"vvv"),("v",5),("s",4),("s",5),("v",7),("s",6),("s",7)]
+PE_CHUNKS = (1, 3, 5, 6)
+GP_CHUNKS = (0, 2, 4, 7)
+ZT = {0: (0, 1), 2: (2, 3), 4: (4, 5), 6: (6, 7)}
+SQ = {0: (0,), 1: (1,), 2: (2,), 3: (3,), 4: (4,), 5: (5,), 6: (6,), 7: (7,)}
+S_WEAVE = ()
+NSPLIT = 5
+HEAD = [("ae",0,"sss"),("v",1),("ae",2,"sss"),("v",3),("s",1),("s",0),("ae",4,"ssv"),("s",2),("s",3),("ae",7,"vvv"),("v",5),("s",4),("s",5),("v",6),("s",7),("s",6)]
 
 
 def tile_endpoint_span_scorer_f1_kernel(
@@ -53,7 +57,7 @@ def tile_endpoint_span_scorer_f1_kernel(
         wesp = keep.tile([P, KG, F], U8, name="wesp", align_bytes=64)
         wv = keep.tile([P, KG, 512], U8, name="wv", align_bytes=64)
         wvs = keep.tile([P, KG, R], U8, name="wvs", align_bytes=64)
-        xt = keep.tile([P, KG, TOK * 4], BF16, name="xt", align_bytes=64)
+        xt = keep.tile([P, KG, TOK * 4], BF16, name="xt", tag="z3", bufs=1, align_bytes=64)
         xc = keep.tile([P, KG, TOK], U32, name="xc", align_bytes=64)
         xp = [keep.tile([P, KG, TOK], U8, name="xp%d" % s, align_bytes=64) for s in range(4)]
         wg = keep.tile([P, F], BF16, name="wg")
@@ -72,8 +76,10 @@ def tile_endpoint_span_scorer_f1_kernel(
             nc.sync.dma_start(out=t[:], in_=x_bytes[:, 8 * m : 8 * m + 8, :].rearrange("b j d -> j b d"))
             xb.append(t)
 
-        def load_words(tile, src):
-            nc.sync.dma_start(out=tile[:].bitcast(I32), in_=src.rearrange("g p n -> p g n").bitcast(I32))
+        def load_words(tile, src, lo, hi):
+            nc.sync.dma_start(
+                out=tile[:, :, lo:hi].bitcast(I32), in_=src[:, :, lo:hi].rearrange("g p n -> p g n").bitcast(I32)
+            )
 
         def load_scales(tile, src):
             for q in range(4):
@@ -90,17 +96,19 @@ def tile_endpoint_span_scorer_f1_kernel(
         make_identity(nc, ident[:])
         nc.scalar.activation(out=warm[:], in_=warm[:], func=ACT.Silu)
 
+        load_words(ws_raw, ws_words, 0, 1024)
+        load_words(we_raw, we_words, 0, 1024)
         for m in range(5):
             load_x(m)
+        load_scales(wss_raw, ws_scales)
+        load_scales(wes_raw, we_scales)
         nc.sync.dma_start(out=wg[0:W, :], in_=width)
         nc.sync.dma_start(out=wg[W : W + 1, :], in_=gain.unsqueeze(0))
-        load_words(we_raw, we_words)
-        load_words(ws_raw, ws_words)
-        load_scales(wes_raw, we_scales)
-        load_scales(wss_raw, ws_scales)
+        load_words(ws_raw, ws_words, 1024, 2048)
+        load_words(we_raw, we_words, 1024, 2048)
         for m in range(5, 9):
             load_x(m)
-        load_words(wv, wv_words)
+        load_words(wv, wv_words, 0, 512)
         load_scales(wvs, wv_scales)
         nc.sync.dma_start(out=pr[:].rearrange("p w r -> p (w r)"), in_=prior.rearrange("w r -> (w r)").partition_broadcast(P))
 
@@ -206,6 +214,14 @@ def tile_endpoint_span_scorer_f1_kernel(
                 op=ALU.add,
             )
 
+        def vadd_all(k):
+            half, w = GROUPS[k]
+            v[k] = work.tile([P, len(GP_CHUNKS), HALF], F32, name="v", tag="v", bufs=2)
+            n0 = HALF * half
+            nc.gpsimd.tensor_tensor(
+                out=v[k][:], in0=a_sb[:, :, n0 : n0 + HALF], in1=e_sb[:, :, n0 + B * w : n0 + B * w + HALF], op=ALU.add
+            )
+
         def vpe(k, c):
             half, w = GROUPS[k]
             bank = psum.tile([P, HALF], F32, name="vp", tag="vp", bufs=2)
@@ -216,7 +232,7 @@ def tile_endpoint_span_scorer_f1_kernel(
         def silu(k, c):
             half, w = GROUPS[k]
             if k not in z:
-                z[k] = work.tile([P, CH, HALF], F32, name="z", tag="z", bufs=3)
+                z[k] = keep.tile([P, CH, HALF], F32, name="z", tag="z%d" % (k % 4), bufs=1, align_bytes=64)
             src = vbank.pop((k, c))[:] if c in PE_CHUNKS else v[k][:, GP_CHUNKS.index(c), :]
             nc.scalar.activation(out=z[k][:, c, :], in_=src, func=ACT.Silu, bias=wid[:, c, w : w + 1])
 
@@ -261,7 +277,7 @@ def tile_endpoint_span_scorer_f1_kernel(
             )
 
         def weave(k, g, eng="v"):
-            if g == 0:
+            if k not in hb:
                 hb[k] = work.tile([P, KG, 4 * HALF], BF16, name="hb", tag="hb", bufs=2, align_bytes=64)
             dst = hb[k][:, g, :].rearrange("p (c i t) -> p c t i", i=4, t=4)
             src = hp[k][:, 4 * g : 4 * g + 4, :].rearrange("p t (c i) -> p c t i", i=4)
@@ -271,7 +287,7 @@ def tile_endpoint_span_scorer_f1_kernel(
                 nc.scalar.copy(out=dst, in_=src)
 
         def quant(k, g):
-            if g == 0:
+            if k not in hc:
                 hc[k] = work.tile([P, KG, HALF], U32, name="hc", tag="hc", bufs=2, align_bytes=64)
                 hs[k] = work.tile([P, KG, HALF], U8, name="hs", tag="hs", bufs=2, align_bytes=64)
             nc.vector.quantize_mx(out=hc[k][:, g, :].bitcast(FP8X4), scales=hs[k][:, g, :], in_=hb[k][:, g, :])
@@ -305,6 +321,8 @@ def tile_endpoint_span_scorer_f1_kernel(
                 i0 = 32 * half + 8 * (2 * jj + j2)
                 nc.sync.dma_start(out=out[:, i0 : i0 + 8, w, :].rearrange("b i r -> i b r"), in_=so[:, j2, :])
 
+        perm_words(wsp, ws_raw, 0)
+        perm_words(wep, we_raw, 0)
         for m in range(5):
             x_prod(m)
             x_turn(m)
@@ -314,10 +332,8 @@ def tile_endpoint_span_scorer_f1_kernel(
             for u in range(2):
                 nc.tensor.transpose(bank[:, 2 * g + u, :], words[:, 256 * g + u : 256 * (g + 1) : 2], ident[:])
         nc.scalar.copy(out=wgt[:], in_=bank[:, :, 0:16].rearrange("p (g u) n -> p g n u", u=2))
-        perm_words(wsp, ws_raw, 0)
         perm_scales(wssp, wss_raw, 0)
         x_quant(0, 512)
-        perm_words(wep, we_raw, 0)
         perm_scales(wesp, wes_raw, 0)
         x_quant(512, 640)
         wgt_bf = wgt[:].rearrange("p g n u -> p (g n u)").bitcast(BF16).rearrange("p (g n t) -> p g n t", g=2, t=4)
@@ -345,41 +361,94 @@ def tile_endpoint_span_scorer_f1_kernel(
             vadd(1, c, nc.vector)
         for m in range(5, 9):
             x_prod(m)
-
-        for k in range(NG + 3):
+        for k in range(NG - 1):
             if ok(k - 1):
                 rstd(k - 1)
             if ok(k + 2):
-                for c in GP_CHUNKS:
-                    vadd(k + 2, c)
-            if ok(k - 3):
-                finish(k - 3, 0)
-                finish(k - 3, 1)
+                vadd_all(k + 2)
+            if ok(k - 2):
+                for c in range(NSPLIT, CH):
+                    norm(k - 2, c)
+            if ok(k - 4):
+                finish(k - 4, 0)
+                finish(k - 4, 1)
             for i in range(8):
-                if ok(k) and i % 2 == 0:
-                    ztr(k, i)
-                    ztr(k, i + 1)
+                if ok(k) and i in ZT:
+                    for b in ZT[i]:
+                        ztr(k, b)
                 if i == 2 and ok(k - 1):
                     spread(k - 1)
-                    for c in range(CH):
+                    for c in range(NSPLIT):
                         norm(k - 1, c)
+                if i == 2 and ok(k - 2):
                     for g in range(KG):
-                        weave(k - 1, g, "s" if k == NG and g == 0 else "v")
+                        weave(k - 2, g)
                     for g in range(KG):
-                        quant(k - 1, g)
-                if i == 5 and ok(k - 2):
-                    outmm(k - 2, 0)
-                    outmm(k - 2, 1)
+                        quant(k - 2, g)
+                if i == 7 and ok(k - 3):
+                    outmm(k - 3, 0)
+                    outmm(k - 3, 1)
                 if ok(k + 1) and i in PE_CHUNKS:
                     vpe(k + 1, i)
                 if k == 0 and i % 2 == 1:
                     x_turn(5 + i // 2)
                 if ok(k):
-                    square(k, i)
+                    for b in SQ[i]:
+                        square(k, b)
                 if ok(k + 1):
                     silu(k + 1, i)
             if k == 1:
                 x_quant(640, 1152)
                 shift_planes(640, 1152)
             if 2 <= k <= 1 + len(GP_CHUNKS):
-                proj_ae(GP_CHUNKS[k - 2], 1, "vs")
+                proj_ae(GP_CHUNKS[k - 2], 1, "ss")
+        k = NG - 1
+        rstd(k - 1)
+        for c in range(NSPLIT, CH):
+            norm(k - 2, c)
+        finish(k - 4, 0)
+        finish(k - 4, 1)
+        for i in range(0, 8, 2):
+            ztr(k, i)
+            ztr(k, i + 1)
+            if i == 2:
+                spread(k - 1)
+                for c in range(NSPLIT):
+                    norm(k - 1, c)
+            if i == 6:
+                outmm(k - 3, 0)
+                outmm(k - 3, 1)
+            square(k, i)
+            square(k, i + 1)
+        weave(k - 2, 0, "s")
+        weave(k - 2, 1)
+        quant(k - 2, 1)
+        rstd(k)
+        quant(k - 2, 0)
+        for c in range(NSPLIT, CH):
+            norm(k - 1, c)
+        weave(k - 1, 0, "s")
+        weave(k - 1, 1, "s")
+        spread(k)
+        finish(k - 3, 0)
+        finish(k - 3, 1)
+        outmm(k - 2, 0)
+        outmm(k - 2, 1)
+        for c in range(CH):
+            norm(k, c)
+        weave(k, 0, "s")
+        quant(k - 1, 0)
+        quant(k - 1, 1)
+        weave(k, 1, "s")
+        finish(k - 2, 0)
+        finish(k - 2, 1)
+        outmm(k - 1, 0)
+        outmm(k - 1, 1)
+        quant(k, 0)
+        quant(k, 1)
+        outmm(k, 0)
+        finish(k - 1, 0)
+        finish(k - 1, 1)
+        outmm(k, 1)
+        finish(k, 0)
+        finish(k, 1)

@@ -29,8 +29,8 @@ GP_CHUNKS = (0, 2, 4, 7)
 ZT = {0: (0, 1), 2: (2, 3), 4: (4, 5), 6: (6, 7)}
 SQ = {0: (0,), 1: (1,), 2: (2,), 3: (3,), 4: (4,), 5: (5,), 6: (6,), 7: (7,)}
 S_WEAVE = ()
-NSPLIT = 5
-HEAD = [("ae",0,"sss"),("v",1),("ae",2,"sss"),("v",3),("s",1),("s",0),("ae",4,"ssv"),("s",2),("s",3),("ae",7,"vvv"),("v",5),("s",4),("s",5),("v",6),("s",7),("s",6)]
+NSPLIT = 6
+HEAD = [("a", 0, "s"), ("a", 2, "s"), ("e", 0, "s"), ("e", 2, "s"), ("+", 0, ""), ("+", 2, ""), ("v", 1, ""), ("v", 3, ""), ("s", 1, ""), ("s", 0, ""), ("s", 3, ""), ("s", 2, ""), ("a", 4, "s"), ("e", 4, "s"), ("+", 4, ""), ("a", 7, "v"), ("e", 7, "v"), ("+", 7, ""), ("v", 5, ""), ("s", 5, ""), ("s", 4, ""), ("v", 6, ""), ("s", 6, ""), ("s", 7, "")]
 
 
 def tile_endpoint_span_scorer_f1_kernel(
@@ -96,10 +96,10 @@ def tile_endpoint_span_scorer_f1_kernel(
         make_identity(nc, ident[:])
         nc.scalar.activation(out=warm[:], in_=warm[:], func=ACT.Silu)
 
-        load_words(ws_raw, ws_words, 0, 1024)
-        load_words(we_raw, we_words, 0, 1024)
         for m in range(5):
             load_x(m)
+        load_words(ws_raw, ws_words, 0, 1024)
+        load_words(we_raw, we_words, 0, 1024)
         load_scales(wss_raw, ws_scales)
         load_scales(wes_raw, we_scales)
         nc.sync.dma_start(out=wg[0:W, :], in_=width)
@@ -124,9 +124,10 @@ def tile_endpoint_span_scorer_f1_kernel(
             for g in range(KG):
                 for u in range(2):
                     nc.tensor.transpose(bank[:, 2 * g + u, :], words[:, 256 * g + u : 256 * (g + 1) : 2], ident[:])
-            nc.scalar.copy(
-                out=xt[:].bitcast(F32)[:, :, 256 * m : 256 * (m + 1)].rearrange("p g (n u) -> p g n u", u=2),
-                in_=bank[:].rearrange("p (g u) n -> p g n u", u=2),
+            evac(
+                "s" if m < 5 else "v",
+                xt[:].bitcast(F32)[:, :, 256 * m : 256 * (m + 1)].rearrange("p g (n u) -> p g n u", u=2),
+                bank[:].rearrange("p (g u) n -> p g n u", u=2),
             )
 
         def x_quant(n0, n1):
@@ -176,16 +177,17 @@ def tile_endpoint_span_scorer_f1_kernel(
             else:
                 nc.vector.tensor_copy(out=dst, in_=src)
 
-        def proj_ae(c, half, engines):
+        def proj_a(c, half, eng, tag="vp"):
             gi = GP_CHUNKS.index(c)
-            spans = [(0, 512), (512, 128)] if half == 0 else [(640, 512)]
-            bank = psum.tile([P, HALF], F32, name="vp", tag="vp", bufs=2)
+            bank = psum.tile([P, HALF], F32, name=tag, tag=tag, bufs=2)
             proj(bank[:], wsp, wssp, c, HALF * half, HALF, 0, True, True)
-            evac(engines[0], a_sb[:, gi, HALF * half : HALF * (half + 1)], bank[:])
-            for i, (n0, n) in enumerate(spans):
-                bank = psum.tile([P, HALF], F32, name="vp", tag="vp", bufs=2)
-                proj(bank[:, :n], wep, wesp, c, n0, n, 0, True, True)
-                evac(engines[1 + i], e_sb[:, gi, n0 : n0 + n], bank[:, :n])
+            evac(eng, a_sb[:, gi, HALF * half : HALF * (half + 1)], bank[:])
+
+        def proj_e(c, n0, n, eng, tag="vp"):
+            gi = GP_CHUNKS.index(c)
+            bank = psum.tile([P, HALF], F32, name=tag, tag=tag, bufs=2)
+            proj(bank[:, :n], wep, wesp, c, n0, n, 0, True, True)
+            evac(eng, e_sb[:, gi, n0 : n0 + n], bank[:, :n])
 
         v = {}
         vbank = {}
@@ -279,8 +281,8 @@ def tile_endpoint_span_scorer_f1_kernel(
         def weave(k, g, eng="v"):
             if k not in hb:
                 hb[k] = work.tile([P, KG, 4 * HALF], BF16, name="hb", tag="hb", bufs=2, align_bytes=64)
-            dst = hb[k][:, g, :].rearrange("p (c i t) -> p c t i", i=4, t=4)
-            src = hp[k][:, 4 * g : 4 * g + 4, :].rearrange("p t (c i) -> p c t i", i=4)
+            dst = hb[k][:, g, :].rearrange("p (n t) -> p n t", t=4)
+            src = hp[k][:, 4 * g : 4 * g + 4, :].rearrange("p t n -> p n t")
             if eng == "v":
                 nc.vector.tensor_copy(out=dst, in_=src)
             else:
@@ -321,8 +323,6 @@ def tile_endpoint_span_scorer_f1_kernel(
                 i0 = 32 * half + 8 * (2 * jj + j2)
                 nc.sync.dma_start(out=out[:, i0 : i0 + 8, w, :].rearrange("b i r -> i b r"), in_=so[:, j2, :])
 
-        perm_words(wsp, ws_raw, 0)
-        perm_words(wep, we_raw, 0)
         for m in range(5):
             x_prod(m)
             x_turn(m)
@@ -332,8 +332,10 @@ def tile_endpoint_span_scorer_f1_kernel(
             for u in range(2):
                 nc.tensor.transpose(bank[:, 2 * g + u, :], words[:, 256 * g + u : 256 * (g + 1) : 2], ident[:])
         nc.scalar.copy(out=wgt[:], in_=bank[:, :, 0:16].rearrange("p (g u) n -> p g n u", u=2))
+        perm_words(wsp, ws_raw, 0)
         perm_scales(wssp, wss_raw, 0)
         x_quant(0, 512)
+        perm_words(wep, we_raw, 0)
         perm_scales(wesp, wes_raw, 0)
         x_quant(512, 640)
         wgt_bf = wgt[:].rearrange("p g n u -> p (g n u)").bitcast(BF16).rearrange("p (g n t) -> p g n t", g=2, t=4)
@@ -348,14 +350,17 @@ def tile_endpoint_span_scorer_f1_kernel(
                 out=g32[:, 4 * g : 4 * g + 4], in0=wgt_bf[:, g, W, :], scalar1=32.0, scalar2=None, op0=ALU.mult
             )
         shift_planes(0, 640)
-        for step in HEAD:
-            c = step[1]
-            if step[0] == "ae":
-                proj_ae(c, 0, step[2])
+        for what, c, eng in HEAD:
+            if what == "a":
+                proj_a(c, 0, eng, "o")
+            if what == "e":
+                proj_e(c, 0, 512, eng)
+                proj_e(c, 512, 128, eng, "o")
+            if what == "+":
                 vadd(0, c, nc.vector)
-            if step[0] == "v":
+            if what == "v":
                 vpe(0, c)
-            if step[0] == "s":
+            if what == "s":
                 silu(0, c)
         for c in GP_CHUNKS:
             vadd(1, c, nc.vector)
@@ -401,7 +406,8 @@ def tile_endpoint_span_scorer_f1_kernel(
                 x_quant(640, 1152)
                 shift_planes(640, 1152)
             if 2 <= k <= 1 + len(GP_CHUNKS):
-                proj_ae(GP_CHUNKS[k - 2], 1, "ss")
+                proj_a(GP_CHUNKS[k - 2], 1, "v")
+                proj_e(GP_CHUNKS[k - 2], 640, 512, "s")
         k = NG - 1
         rstd(k - 1)
         for c in range(NSPLIT, CH):
@@ -439,7 +445,7 @@ def tile_endpoint_span_scorer_f1_kernel(
         weave(k, 0, "s")
         quant(k - 1, 0)
         quant(k - 1, 1)
-        weave(k, 1, "s")
+        weave(k, 1)
         finish(k - 2, 0)
         finish(k - 2, 1)
         outmm(k - 1, 0)

from contextlib import ExitStack

import concourse.mybir as mybir
from concourse.masks import make_identity

F32 = mybir.dt.float32
BF16 = mybir.dt.bfloat16
I32 = mybir.dt.int32
U32 = mybir.dt.uint32
U8 = mybir.dt.uint8
FP8 = mybir.dt.float8_e4m3fn
FP8X4 = mybir.dt.float8_e4m3fn_x4
FP4X4 = mybir.dt.float4_e2m1fn_x4
ACT = mybir.ActivationFunctionType
ALU = mybir.AluOpType

B, S, L, W, D, F, R = 16, 64, 72, 9, 1024, 1024, 256
FLOPS = 2 * (B * S * D * F + B * L * D * F + B * S * W * F * R)

P = 128
KG = 2
CH = 8
TOK = L * B
HALF = 512
GROUPS = [(h, w) for h in range(2) for w in range(W)]
NG = len(GROUPS)
PE_CHUNKS = (1, 3, 5, 6)
GP_CHUNKS = (0, 2, 4, 7)
ZT = {0: (0, 1), 2: (2, 3), 4: (4, 5), 6: (6, 7)}
SQ = {0: (0,), 1: (1,), 2: (2,), 3: (3,), 4: (4,), 5: (5,), 6: (6,), 7: (7,)}
S_WEAVE = ()
NSPLIT = 6
HEAD = [("a", 0, "s"), ("a", 2, "s"), ("e", 0, "s"), ("e", 2, "s"), ("+", 0, ""), ("+", 2, ""), ("v", 1, ""), ("v", 3, ""), ("s", 1, ""), ("s", 0, ""), ("s", 3, ""), ("s", 2, ""), ("a", 4, "s"), ("e", 4, "s"), ("+", 4, ""), ("a", 7, "v"), ("e", 7, "v"), ("+", 7, ""), ("v", 5, ""), ("s", 5, ""), ("s", 4, ""), ("v", 6, ""), ("s", 6, ""), ("s", 7, "")]


def tile_endpoint_span_scorer_f1_kernel(
    tc, x_bytes, x_scale, ws_words, ws_scales, we_words, we_scales, width, gain, wv_words, wv_scales, prior, out
):
    nc = tc.nc
    with ExitStack() as ctx:
        keep = ctx.enter_context(tc.tile_pool(name="keep", bufs=1))
        work = ctx.enter_context(tc.tile_pool(name="work", bufs=2))
        psum = ctx.enter_context(tc.psum_pool(name="psum", bufs=1))
        ctx.enter_context(tc.manual_schedule())

        ident = keep.tile([P, P], F32, name="ident")
        warm = keep.tile([P, 1], F32, name="warm")
        mhalf = keep.tile([P, 4], F32, name="mhalf")
        xsc = keep.tile([P, D], F32, name="xsc")
        ws_raw = keep.tile([P, KG, 2048], U8, name="ws_raw")
        we_raw = keep.tile([P, KG, 2048], U8, name="we_raw")
        wss_raw = keep.tile([P, KG, F], U8, name="wss_raw")
        wes_raw = keep.tile([P, KG, F], U8, name="wes_raw")
        wsp = keep.tile([P, KG, 2048], U8, name="wsp", align_bytes=64)
        wep = keep.tile([P, KG, 2048], U8, name="wep", align_bytes=64)
        wssp = keep.tile([P, KG, F], U8, name="wssp", align_bytes=64)
        wesp = keep.tile([P, KG, F], U8, name="wesp", align_bytes=64)
        wv = keep.tile([P, KG, 512], U8, name="wv", align_bytes=64)
        wvs = keep.tile([P, KG, R], U8, name="wvs", align_bytes=64)
        xt = keep.tile([P, KG, TOK * 4], BF16, name="xt", tag="z3", bufs=1, align_bytes=64)
        xc = keep.tile([P, KG, TOK], U32, name="xc", align_bytes=64)
        xp = [keep.tile([P, KG, TOK], U8, name="xp%d" % s, align_bytes=64) for s in range(4)]
        wg = keep.tile([P, F], BF16, name="wg")
        wgt = keep.tile([P, KG, 16, 2], F32, name="wgt")
        wid = keep.tile([P, CH, W], F32, name="wid")
        g32 = keep.tile([P, CH], F32, name="g32")
        pr = keep.tile([P, W, R], BF16, name="pr")
        a_sb = keep.tile([P, len(GP_CHUNKS), S * B], F32, name="a_sb")
        e_sb = keep.tile([P, len(GP_CHUNKS), TOK], F32, name="e_sb")

        nc.scalar.dma_start(out=xsc[:], in_=x_scale.rearrange("a o k -> (a o k)").partition_broadcast(P))
        xb = []

        def load_x(m):
            t = keep.tile([P, D], U8, name="xb%d" % m)
            nc.sync.dma_start(out=t[:], in_=x_bytes[:, 8 * m : 8 * m + 8, :].rearrange("b j d -> j b d"))
            xb.append(t)

        def load_words(tile, src, lo, hi):
            nc.sync.dma_start(
                out=tile[:, :, lo:hi].bitcast(I32), in_=src[:, :, lo:hi].rearrange("g p n -> p g n").bitcast(I32)
            )

        def load_scales(tile, src):
            for q in range(4):
                nc.sync.dma_start(
                    out=tile[32 * q : 32 * q + 4, :, :].bitcast(I32),
                    in_=src[:, 4 * q : 4 * q + 4, :].rearrange("g q n -> q g n").bitcast(I32),
                )

        for t in (wss_raw, wes_raw, wvs, xp[0]):
            nc.vector.memset(t[:].bitcast(I32), 0)
        nc.gpsimd.memset(warm[:], 0.0)
        nc.gpsimd.memset(mhalf[:], -0.5)
        nc.gpsimd.memset(wg[:], 0.0)
        make_identity(nc, ident[:])
        nc.scalar.activation(out=warm[:], in_=warm[:], func=ACT.Silu)

        for m in range(5):
            load_x(m)
        load_words(ws_raw, ws_words, 0, 1024)
        load_words(we_raw, we_words, 0, 1024)
        load_scales(wss_raw, ws_scales)
        load_scales(wes_raw, we_scales)
        nc.sync.dma_start(out=wg[0:W, :], in_=width)
        nc.sync.dma_start(out=wg[W : W + 1, :], in_=gain.unsqueeze(0))
        load_words(ws_raw, ws_words, 1024, 2048)
        load_words(we_raw, we_words, 1024, 2048)
        for m in range(5, 9):
            load_x(m)
        load_words(wv, wv_words, 0, 512)
        load_scales(wvs, wv_scales)
        nc.sync.dma_start(out=pr[:].rearrange("p w r -> p (w r)"), in_=prior.rearrange("w r -> (w r)").partition_broadcast(P))

        xs = {}

        def x_prod(m):
            xs[m] = work.tile([P, D], BF16, name="xs", tag="xs", bufs=4)
            nc.vector.tensor_tensor(out=xs[m][:], in0=xb[m][:].bitcast(FP8), in1=xsc[:], op=ALU.mult)

        def x_turn(m):
            words = xs.pop(m)[:].bitcast(F32)
            bank = psum.tile([P, 4, P], F32, name="o", tag="o", bufs=2)
            for g in range(KG):
                for u in range(2):
                    nc.tensor.transpose(bank[:, 2 * g + u, :], words[:, 256 * g + u : 256 * (g + 1) : 2], ident[:])
            evac(
                "s" if m < 5 else "v",
                xt[:].bitcast(F32)[:, :, 256 * m : 256 * (m + 1)].rearrange("p g (n u) -> p g n u", u=2),
                bank[:].rearrange("p (g u) n -> p g n u", u=2),
            )

        def x_quant(n0, n1):
            for g in range(KG):
                nc.vector.quantize_mx(
                    out=xc[:, g, n0:n1].bitcast(FP8X4),
                    scales=xp[0][:, g, n0:n1],
                    in_=xt[:, g, 4 * n0 : 4 * n1],
                )

        def shift_planes(n0, n1):
            for s in range(1, 4):
                lo = max(n0, 16 * s)
                nc.vector.tensor_copy(
                    out=xp[s][:, :, lo - 16 * s : n1 - 16 * s].bitcast(I32),
                    in_=xp[0][:, :, lo:n1].bitcast(I32),
                )

        def perm_words(dst, src, fg):
            for g in range(KG):
                nc.vector.tensor_copy(
                    out=dst[:, g, 1024 * fg : 1024 * (fg + 1)].rearrange("p (t m b) -> p t m b", t=4, b=2),
                    in_=src[:, g, 1024 * fg : 1024 * (fg + 1)].rearrange("p (m t b) -> p t m b", t=4, b=2),
                )

        def perm_scales(dst, src, fg):
            nc.vector.tensor_copy(
                out=dst[:, :, 512 * fg : 512 * (fg + 1)].rearrange("p g (t m) -> p g t m", t=4),
                in_=src[:, :, 512 * fg : 512 * (fg + 1)].rearrange("p g (m t) -> p g t m", t=4),
            )

        def proj(bank, words, scales, c, n0, n, plane, first, last):
            for g in range(KG):
                nc.tensor.matmul_mx(
                    out=bank,
                    lhsT=words[:, g, 256 * c : 256 * (c + 1)].bitcast(FP4X4),
                    lhsT_scale=scales[:, g, P * c : P * (c + 1)],
                    rhs=xc[:, g, n0 : n0 + n].bitcast(FP8X4),
                    rhs_scale=xp[plane][:, g, n0 - 16 * plane : n0 - 16 * plane + n],
                    start=(first and g == 0),
                    stop=(last and g == KG - 1),
                )

        def evac(eng, dst, src):
            if eng == "s":
                nc.scalar.copy(out=dst, in_=src)
            else:
                nc.vector.tensor_copy(out=dst, in_=src)

        def proj_a(c, half, eng, tag="vp"):
            gi = GP_CHUNKS.index(c)
            bank = psum.tile([P, HALF], F32, name=tag, tag=tag, bufs=2)
            proj(bank[:], wsp, wssp, c, HALF * half, HALF, 0, True, True)
            evac(eng, a_sb[:, gi, HALF * half : HALF * (half + 1)], bank[:])

        def proj_e(c, n0, n, eng, tag="vp"):
            gi = GP_CHUNKS.index(c)
            bank = psum.tile([P, HALF], F32, name=tag, tag=tag, bufs=2)
            proj(bank[:, :n], wep, wesp, c, n0, n, 0, True, True)
            evac(eng, e_sb[:, gi, n0 : n0 + n], bank[:, :n])

        v = {}
        vbank = {}
        z = {}
        ss = {}
        rb = {}
        rs = {}
        hb = {}
        hp = {}
        hc = {}
        hs = {}

        def ok(k):
            return 0 <= k < NG

        def vadd(k, c, eng=nc.gpsimd):
            half, w = GROUPS[k]
            gi = GP_CHUNKS.index(c)
            if gi == 0:
                v[k] = work.tile([P, len(GP_CHUNKS), HALF], F32, name="v", tag="v", bufs=2)
            n0 = HALF * half
            eng.tensor_tensor(
                out=v[k][:, gi, :],
                in0=a_sb[:, gi, n0 : n0 + HALF],
                in1=e_sb[:, gi, n0 + B * w : n0 + B * w + HALF],
                op=ALU.add,
            )

        def vadd_all(k):
            half, w = GROUPS[k]
            v[k] = work.tile([P, len(GP_CHUNKS), HALF], F32, name="v", tag="v", bufs=2)
            n0 = HALF * half
            nc.gpsimd.tensor_tensor(
                out=v[k][:], in0=a_sb[:, :, n0 : n0 + HALF], in1=e_sb[:, :, n0 + B * w : n0 + B * w + HALF], op=ALU.add
            )

        def vpe(k, c):
            half, w = GROUPS[k]
            bank = psum.tile([P, HALF], F32, name="vp", tag="vp", bufs=2)
            proj(bank[:], wsp, wssp, c, HALF * half, HALF, 0, True, False)
            proj(bank[:], wep, wesp, c, HALF * half + B * w, HALF, w % 4, False, True)
            vbank[k, c] = bank

        def silu(k, c):
            half, w = GROUPS[k]
            if k not in z:
                z[k] = keep.tile([P, CH, HALF], F32, name="z", tag="z%d" % (k % 4), bufs=1, align_bytes=64)
            src = vbank.pop((k, c))[:] if c in PE_CHUNKS else v[k][:, GP_CHUNKS.index(c), :]
            nc.scalar.activation(out=z[k][:, c, :], in_=src, func=ACT.Silu, bias=wid[:, c, w : w + 1])

        zbank = {}

        def ztr(k, i):
            q, j = divmod(i, 4)
            bank = psum.tile([P, 4, P], F32, name="zt", tag="zt", bufs=3)
            for t in range(4):
                nc.tensor.transpose(bank[:, t, :], z[k][:, 4 * q + t, P * j : P * (j + 1)], ident[:])
            zbank[k, i] = bank

        def square(k, i):
            q, j = divmod(i, 4)
            if i == 0:
                ss[k] = work.tile([P, 2, 4], F32, name="ss", tag="ss", bufs=3)
            junk = work.tile([P, HALF], BF16, name="junk", tag="junk", bufs=2)
            nc.scalar.activation(
                out=junk[:],
                in_=zbank.pop((k, i))[:].rearrange("p t n -> p (t n)"),
                func=ACT.Square,
                accum_out=ss[k][:, q, j : j + 1],
            )

        def rstd(k):
            tot = work.tile([P, 4], F32, name="tot", tag="tot", bufs=2)
            nc.vector.tensor_tensor(out=tot[:], in0=ss[k][:, 0, :], in1=ss[k][:, 1, :], op=ALU.add)
            rs[k] = work.tile([P, 4], F32, name="rs", tag="rs", bufs=2)
            nc.gpsimd.tensor_tensor(out=rs[k][:], in0=tot[:], in1=mhalf[:], op=ALU.pow)

        def spread(k):
            bank = psum.tile([P, HALF], F32, name="rb", tag="rb", bufs=1)
            for j in range(4):
                nc.tensor.transpose(bank[:, P * j : P * (j + 1)], rs[k][:, j : j + 1].to_broadcast([P, P]), ident[:])
            rb[k] = bank

        def norm(k, c):
            if c == 0:
                hp[k] = work.tile([P, CH, HALF], BF16, name="hp", tag="hp", bufs=2)
            nc.vector.scalar_tensor_tensor(
                out=hp[k][:, c, :], in0=z[k][:, c, :], scalar=g32[:, c : c + 1], in1=rb[k][:], op0=ALU.mult, op1=ALU.mult
            )

        def weave(k, g, eng="v"):
            if k not in hb:
                hb[k] = work.tile([P, KG, 4 * HALF], BF16, name="hb", tag="hb", bufs=2, align_bytes=64)
            dst = hb[k][:, g, :].rearrange("p (n t) -> p n t", t=4)
            src = hp[k][:, 4 * g : 4 * g + 4, :].rearrange("p t n -> p n t")
            if eng == "v":
                nc.vector.tensor_copy(out=dst, in_=src)
            else:
                nc.scalar.copy(out=dst, in_=src)

        def quant(k, g):
            if k not in hc:
                hc[k] = work.tile([P, KG, HALF], U32, name="hc", tag="hc", bufs=2, align_bytes=64)
                hs[k] = work.tile([P, KG, HALF], U8, name="hs", tag="hs", bufs=2, align_bytes=64)
            nc.vector.quantize_mx(out=hc[k][:, g, :].bitcast(FP8X4), scales=hs[k][:, g, :], in_=hb[k][:, g, :])

        obank = {}

        def outmm(k, jj):
            bank = psum.tile([P, 2, R], F32, name="o", tag="o", bufs=2)
            for j2 in range(2):
                j = 2 * jj + j2
                for rh in range(2):
                    for g in range(KG):
                        nc.tensor.matmul_mx(
                            out=bank[:, j2, P * rh : P * (rh + 1)],
                            lhsT=hc[k][:, g, P * j : P * (j + 1)].bitcast(FP8X4),
                            lhsT_scale=hs[k][:, g, P * j : P * (j + 1)],
                            rhs=wv[:, g, 2 * P * rh : 2 * P * (rh + 1)].bitcast(FP4X4),
                            rhs_scale=wvs[:, g, P * rh : P * (rh + 1)],
                            start=(g == 0),
                            stop=(g == KG - 1),
                        )
            obank[k, jj] = bank

        def finish(k, jj):
            half, w = GROUPS[k]
            so = work.tile([P, 2, R], F32, name="so", tag="so", bufs=3)
            nc.vector.tensor_tensor(
                out=so[:], in0=obank.pop((k, jj))[:], in1=pr[:, w, :].unsqueeze(1).to_broadcast([P, 2, R]), op=ALU.add
            )
            for j2 in range(2):
                i0 = 32 * half + 8 * (2 * jj + j2)
                nc.sync.dma_start(out=out[:, i0 : i0 + 8, w, :].rearrange("b i r -> i b r"), in_=so[:, j2, :])

        for m in range(5):
            x_prod(m)
            x_turn(m)
        bank = psum.tile([P, 4, P], F32, name="zt", tag="zt", bufs=3)
        words = wg[:].bitcast(F32)
        for g in range(KG):
            for u in range(2):
                nc.tensor.transpose(bank[:, 2 * g + u, :], words[:, 256 * g + u : 256 * (g + 1) : 2], ident[:])
        nc.scalar.copy(out=wgt[:], in_=bank[:, :, 0:16].rearrange("p (g u) n -> p g n u", u=2))
        perm_words(wsp, ws_raw, 0)
        perm_scales(wssp, wss_raw, 0)
        x_quant(0, 512)
        perm_words(wep, we_raw, 0)
        perm_scales(wesp, wes_raw, 0)
        x_quant(512, 640)
        wgt_bf = wgt[:].rearrange("p g n u -> p (g n u)").bitcast(BF16).rearrange("p (g n t) -> p g n t", g=2, t=4)
        for g in range(KG):
            nc.vector.tensor_copy(out=wid[:, 4 * g : 4 * g + 4, :], in_=wgt_bf[:, g, 0:W, :].rearrange("p n t -> p t n"))
        perm_words(wsp, ws_raw, 1)
        perm_scales(wssp, wss_raw, 1)
        perm_words(wep, we_raw, 1)
        perm_scales(wesp, wes_raw, 1)
        for g in range(KG):
            nc.vector.tensor_scalar(
                out=g32[:, 4 * g : 4 * g + 4], in0=wgt_bf[:, g, W, :], scalar1=32.0, scalar2=None, op0=ALU.mult
            )
        shift_planes(0, 640)
        for what, c, eng in HEAD:
            if what == "a":
                proj_a(c, 0, eng, "o")
            if what == "e":
                proj_e(c, 0, 512, eng)
                proj_e(c, 512, 128, eng, "o")
            if what == "+":
                vadd(0, c, nc.vector)
            if what == "v":
                vpe(0, c)
            if what == "s":
                silu(0, c)
        for c in GP_CHUNKS:
            vadd(1, c, nc.vector)
        for m in range(5, 9):
            x_prod(m)
        for k in range(NG - 1):
            if ok(k - 1):
                rstd(k - 1)
            if ok(k + 2):
                vadd_all(k + 2)
            if ok(k - 2):
                for c in range(NSPLIT, CH):
                    norm(k - 2, c)
            if ok(k - 4):
                finish(k - 4, 0)
                finish(k - 4, 1)
            for i in range(8):
                if ok(k) and i in ZT:
                    for b in ZT[i]:
                        ztr(k, b)
                if i == 2 and ok(k - 1):
                    spread(k - 1)
                    for c in range(NSPLIT):
                        norm(k - 1, c)
                if i == 2 and ok(k - 2):
                    for g in range(KG):
                        weave(k - 2, g)
                    for g in range(KG):
                        quant(k - 2, g)
                if i == 7 and ok(k - 3):
                    outmm(k - 3, 0)
                    outmm(k - 3, 1)
                if ok(k + 1) and i in PE_CHUNKS:
                    vpe(k + 1, i)
                if k == 0 and i % 2 == 1:
                    x_turn(5 + i // 2)
                if ok(k):
                    for b in SQ[i]:
                        square(k, b)
                if ok(k + 1):
                    silu(k + 1, i)
            if k == 1:
                x_quant(640, 1152)
                shift_planes(640, 1152)
            if 2 <= k <= 1 + len(GP_CHUNKS):
                proj_a(GP_CHUNKS[k - 2], 1, "v")
                proj_e(GP_CHUNKS[k - 2], 640, 512, "s")
        k = NG - 1
        rstd(k - 1)
        for c in range(NSPLIT, CH):
            norm(k - 2, c)
        finish(k - 4, 0)
        finish(k - 4, 1)
        for i in range(0, 8, 2):
            ztr(k, i)
            ztr(k, i + 1)
            if i == 2:
                spread(k - 1)
                for c in range(NSPLIT):
                    norm(k - 1, c)
            if i == 6:
                outmm(k - 3, 0)
                outmm(k - 3, 1)
            square(k, i)
            square(k, i + 1)
        weave(k - 2, 0, "s")
        weave(k - 2, 1)
        quant(k - 2, 1)
        rstd(k)
        quant(k - 2, 0)
        for c in range(NSPLIT, CH):
            norm(k - 1, c)
        weave(k - 1, 0, "s")
        weave(k - 1, 1, "s")
        spread(k)
        finish(k - 3, 0)
        finish(k - 3, 1)
        outmm(k - 2, 0)
        outmm(k - 2, 1)
        for c in range(CH):
            norm(k, c)
        weave(k, 0, "s")
        quant(k - 1, 0)
        quant(k - 1, 1)
        weave(k, 1)
        finish(k - 2, 0)
        finish(k - 2, 1)
        outmm(k - 1, 0)
        outmm(k - 1, 1)
        quant(k, 0)
        quant(k, 1)
        outmm(k, 0)
        finish(k - 1, 0)
        finish(k - 1, 1)
        outmm(k, 1)
        finish(k, 0)
        finish(k, 1)
